import numpy as np
import ml_dtypes


def mxq(x, axis, fmt="e4m3"):
    dtype, down = {"e4m3": (ml_dtypes.float8_e4m3fn, 7), "e5m2": (ml_dtypes.float8_e5m2, 14)}[fmt]
    v = np.moveaxis(np.asarray(x, np.float32).astype(ml_dtypes.bfloat16).astype(np.float64), axis, -1)
    blocks = v.reshape(v.shape[:-1] + (-1, 32))
    amax = np.abs(blocks).max(-1, keepdims=True)
    byte = np.maximum(np.where(amax > 0, np.frexp(amax)[1] - 1 + 127, 0) - down, 1)
    scale = np.exp2(byte - 127.0)
    codes = (blocks / scale).astype(np.float32).astype(dtype).astype(np.float64)
    return np.moveaxis((codes * scale).reshape(v.shape), -1, axis)


WIDE = False


def mx_kscale(k):
    if not WIDE:
        return np.ones(k)
    levels = np.array([30, -30])
    if k % 512:
        return np.exp2(np.random.permutation(np.resize(levels, k // 32))).repeat(32)
    a = np.empty((k // 512, 16))
    for p in range(k // 512):
        a[p, :8] = np.random.permutation(np.resize(levels, 8))
        for g in range(8):
            far = levels[np.abs(levels - a[p, g]) >= 10]
            a[p, g + 8] = far[np.random.randint(len(far))]
    return np.exp2(a.ravel()).repeat(32)


def f64(x):
    return np.asarray(x).astype(np.float64)


def striped(idx):
    return np.tile(np.asarray(idx).reshape(-1, 16).T, (8, 1)).astype(np.uint16)


def unstriped(offs):
    return offs[:16].T.reshape(-1).astype(np.int64)


E2M1 = np.array([0.0, 0.5, 1.0, 1.5, 2.0, 3.0, 4.0, 6.0, -0.0, -0.5, -1.0, -1.5, -2.0, -3.0, -4.0, -6.0])


def pack_weight(w, fmt):
    k, n = w.shape
    w = f64(np.asarray(w, np.float32).astype(ml_dtypes.bfloat16)).reshape(k // 32, 32, n)
    amax = np.abs(w).max(1)
    if fmt in ("e4m3", "e5m2"):
        byte = np.frexp(amax)[1] - 1 + 127 - (7 if fmt == "e4m3" else 14)
    else:
        mant, ex = np.frexp(amax / 6.0)
        byte = np.where(mant > 0.5, ex, ex - 1) + 127
    byte = np.clip(np.where(amax > 0, byte, 1), 1, 254)
    scaled = (w * np.exp2(127.0 - byte)[:, None, :]).reshape(k, n).astype(np.float32)
    by_word = np.ascontiguousarray(scaled.reshape(k // 512, 128, 4, n).transpose(0, 1, 3, 2))
    if fmt in ("e4m3", "e5m2"):
        words = by_word.astype(ml_dtypes.float8_e4m3fn if fmt == "e4m3" else ml_dtypes.float8_e5m2).view(np.uint8)
    else:
        c = by_word.astype(ml_dtypes.float4_e2m1fn).view(np.uint8) & 0xF
        words = (c[..., 0::2] | (c[..., 1::2] << 4)).reshape(k // 512, 128, 2 * n)
    return np.ascontiguousarray(words), np.ascontiguousarray(byte.astype(np.uint8).reshape(k // 512, 16, n))


def unpack_weight(words, scales, fmt):
    g, _, n = scales.shape
    words = np.ascontiguousarray(words).reshape(g, 128, n, -1)
    if fmt in ("e4m3", "e5m2"):
        vals = words.view(ml_dtypes.float8_e4m3fn if fmt == "e4m3" else ml_dtypes.float8_e5m2).astype(np.float64)
    else:
        nib = np.empty((g, 128, n, 4), np.uint8)
        nib[..., 0::2] = words & 0xF
        nib[..., 1::2] = words >> 4
        vals = E2M1[nib]
    vals = vals * np.repeat(np.exp2(scales.astype(np.float64) - 127.0), 8, axis=1)[..., None]
    return vals.transpose(0, 1, 3, 2).reshape(g * 512, n)


def sigmoid(v):
    return 1.0 / (1.0 + np.exp(-v))


K, T, J, I, L, S, R, C, N = 512, 512, 256, 128, 128, 512, 512, 1024, 256


def setup_inputs():
    n = np.random.standard_normal
    idx = np.random.permutation(T)[:I]
    idx2 = np.random.permutation(S)[:L]
    idx3 = np.random.permutation(C)[:R]
    fk = mx_kscale(K)
    fr = mx_kscale(R)
    wp = pack_weight(n((K, R)) * 1 / np.sqrt(K) * fk[:, None], "e2m1")
    wbp = pack_weight(n((R, N)) * np.random.uniform(0.3, 1.7, (1, N)) / np.sqrt(R) / fr[:, None], "e5m2")
    return {
        "xa": (n((K, T)) / fk[:, None]).astype(np.float32),
        "xb": (n((K, S)) * 0.6 / fk[:, None]).astype(np.float32),
        "w_words": wp[0],
        "w_scales": wp[1],
        "us": (np.random.uniform(0.5, 1.5, (1, R)) * fr).astype(np.float32),
        "tg": (1.0 * n((J, C))).astype(np.float32),
        "wb_words": wbp[0],
        "wb_scales": wbp[1],
        "rs": (0.6 * n((N, J)) * np.random.uniform(0.2, 2.5, (N, 1)) + np.random.uniform(-1.0, 1.0, (N, 1))).astype(np.float32),
        "offs": striped(idx),
        "offs2": striped(idx2),
        "offs3": striped(idx3),
    }


def reference(xa, xb, w_words, w_scales, us, tg, wb_words, wb_scales, rs, offs, offs2, offs3):
    idx = unstriped(offs)
    idx2 = unstriped(offs2)
    idx3 = unstriped(offs3)
    wu = unpack_weight(w_words, w_scales, "e2m1")
    wbu = unpack_weight(wb_words, wb_scales, "e5m2")
    u = np.concatenate([f64(xa)[:, idx], f64(xb)[:, idx2]], axis=1)
    uq = mxq(u, 0, "e4m3")
    a = uq.T @ wu
    hr = a * sigmoid(f64(tg)[:, idx3]) * f64(us)
    hid = hr.T
    hidq = mxq(hid, 0, "e5m2")
    p = wbu.T @ hidq
    pb = p + f64(rs)
    mn = np.mean(pb, axis=1, keepdims=True)
    d = pb - mn
    y = d / np.sqrt(np.mean(np.square(d), axis=1, keepdims=True) + 0.1)
    return y

@@ -1,0 +1,195 @@
+from contextlib import ExitStack
+
+import concourse.mybir as mybir
+from concourse.masks import make_identity
+
+K, T, J, R, C, N = 512, 512, 256, 512, 1024, 256
+FLOPS = 2 * K * J * R + 2 * R * N * J
+
+F32 = mybir.dt.float32
+BF16 = mybir.dt.bfloat16
+I32 = mybir.dt.int32
+U32 = mybir.dt.uint32
+U16 = mybir.dt.uint16
+U8 = mybir.dt.uint8
+E4M3 = mybir.dt.float8_e4m3fn_x4
+E5M2 = mybir.dt.float8_e5m2_x4
+E2M1 = mybir.dt.float4_e2m1fn_x4
+ALU = mybir.AluOpType
+ACT = mybir.ActivationFunctionType
+
+P = 128
+PACK = 4
+HALF = 128
+EPS = 0.1
+
+
+def tile_list_rows_joined_tabled_levelled_kernel(
+    tc, xa, xb, w_words, w_scales, us, tg, wb_words, wb_scales, rs, offs, offs2, offs3, out
+):
+    nc = tc.nc
+    with ExitStack() as ctx:
+        sb = ctx.enter_context(tc.tile_pool(name="sb", bufs=1))
+        ps = ctx.enter_context(tc.psum_pool(name="ps", bufs=1))
+
+        list_a = sb.tile([P, HALF // 16], U16, name="list_a")
+        list_b = sb.tile([P, HALF // 16], U16, name="list_b")
+        list_g = sb.tile([P, R // 16], U16, name="list_g")
+        gates = [sb.tile([P, C], F32, name="gates%d" % h) for h in range(2)]
+        w_raw = sb.tile([P, 2 * R], U8, name="w_raw")
+        w_scale_raw = sb.tile([P, R], U8, name="w_scale_raw")
+        w_codes = sb.tile([P, 2 * R], U8, name="w_codes", align_bytes=64)
+        w_scale = sb.tile([P, R], U8, name="w_scale", align_bytes=64)
+        wb_codes = sb.tile([P, N], U32, name="wb_codes", align_bytes=64)
+        wb_scale = sb.tile([P, N], U8, name="wb_scale", align_bytes=64)
+        factor = sb.tile([P, PACK], F32, name="factor")
+        residual = sb.tile([P, 2, J], F32, name="residual")
+        identity = sb.tile([P, P], F32, name="identity")
+
+        xa_rows = xa.rearrange("(p i) t -> p i t", i=PACK)
+        xb_rows = xb.rearrange("(p i) t -> p i t", i=PACK)
+        windows = [[], []]
+
+        def load_planes(h, rows, first, count):
+            tile = sb.tile([P, count, T], F32, name="x%d_%d" % (h, first))
+            nc.sync.dma_start(out=tile[:], in_=rows[:, first : first + count, :])
+            for i in range(count):
+                windows[h].append(tile[:, i, :])
+
+        def load_scale_rows(plane, rows):
+            for q in range(4):
+                nc.sync.dma_start(
+                    out=plane[32 * q : 32 * q + 4, :].bitcast(I32), in_=rows[0, 4 * q : 4 * q + 4, :].bitcast(I32)
+                )
+
+        nc.gpsimd.memset(w_scale_raw[:].bitcast(I32), 0)
+        nc.gpsimd.memset(wb_scale[:].bitcast(I32), 0)
+        make_identity(nc, identity[:])
+
+        nc.gpsimd.dma_start(out=factor[:], in_=us.rearrange("o (p t) -> p (o t)", t=PACK))
+        nc.sync.dma_start(list_g[:], offs3)
+        nc.sync.dma_start(out=gates[0][:], in_=tg[0:HALF, :])
+        load_scale_rows(w_scale_raw, w_scales)
+        nc.sync.dma_start(list_a[:], offs)
+        load_planes(0, xa_rows, 0, 2)
+        load_planes(0, xa_rows, 2, 2)
+        nc.sync.dma_start(out=w_raw[:].bitcast(I32), in_=w_words[0].bitcast(I32))
+        nc.sync.dma_start(out=gates[1][:], in_=tg[HALF:J, :])
+        nc.sync.dma_start(list_b[:], offs2)
+        load_planes(1, xb_rows, 0, 2)
+        load_planes(1, xb_rows, 2, 1)
+        load_planes(1, xb_rows, 3, 1)
+        nc.sync.dma_start(
+            out=wb_codes[:].bitcast(I32), in_=wb_words[0].rearrange("p n t -> p (n t)").bitcast(I32)
+        )
+        load_scale_rows(wb_scale, wb_scales)
+        nc.sync.dma_start(out=residual[:], in_=rs.rearrange("(a p) j -> p a j", p=P))
+
+        summed = sb.tile([P, 2, J], F32, name="summed")
+        stats = sb.tile([P, 2, 2, 6], F32, name="stats")
+        lists = [list_a, list_b]
+
+        def gate(h):
+            sig = sb.tile([P, R], F32, name="sig%d" % h)
+            nc.scalar.activation(sig[:], gates[h][:].indirect(list_g[:]), ACT.Sigmoid)
+            turned = ps.tile([P, PACK, HALF], F32, name="turned%d" % h)
+            for t in range(PACK):
+                nc.tensor.transpose(turned[:, t, :], sig[:, t:R:PACK], identity[:])
+            return turned
+
+        def scale_gate(h, turned):
+            scaled = sb.tile([P, HALF, PACK], F32, name="scaled%d" % h, tag="shared%d" % h, align_bytes=64)
+            nc.vector.tensor_tensor(
+                scaled[:],
+                turned[:].rearrange("p t j -> p j t"),
+                factor[:].unsqueeze(1).to_broadcast([P, HALF, PACK]),
+                ALU.mult,
+            )
+            return scaled
+
+        def first_product(h):
+            u = sb.tile([P, HALF, PACK], BF16, name="u%d" % h, tag="shared%d" % h, align_bytes=64)
+            for i in range(PACK):
+                nc.vector.tensor_copy(u[:, :, i], windows[h][i].indirect(lists[h][:]))
+            u_codes = sb.tile([P, HALF], U32, name="u_codes%d" % h, align_bytes=64)
+            u_scale = sb.tile([P, HALF], U8, name="u_scale%d" % h, align_bytes=64)
+            nc.vector.quantize_mx(
+                out=u_codes[:].bitcast(E4M3), scales=u_scale[:], in_=u[:].rearrange("p j i -> p (j i)")
+            )
+            a = ps.tile([P, PACK, HALF], F32, name="a%d" % h)
+            for t in range(PACK):
+                nc.tensor.matmul_mx(
+                    out=a[:, t, :],
+                    lhsT=w_codes[:, 2 * P * t : 2 * P * (t + 1)].bitcast(E2M1),
+                    lhsT_scale=w_scale[:, P * t : P * (t + 1)],
+                    rhs=u_codes[:].bitcast(E4M3),
+                    rhs_scale=u_scale[:],
+                    start=True,
+                    stop=True,
+                )
+            return a
+
+        def second_product(h, a, scaled):
+            hid = sb.tile([P, HALF, PACK], BF16, name="hid%d" % h, align_bytes=64)
+            nc.vector.tensor_tensor(hid[:], a[:].rearrange("p t j -> p j t"), scaled[:], ALU.mult)
+            hid_codes = sb.tile([P, HALF], U32, name="hid_codes%d" % h, align_bytes=64)
+            hid_scale = sb.tile([P, HALF], U8, name="hid_scale%d" % h, align_bytes=64)
+            nc.vector.quantize_mx(
+                out=hid_codes[:].bitcast(E5M2), scales=hid_scale[:], in_=hid[:].rearrange("p j t -> p (j t)")
+            )
+            prod = ps.tile([P, 2, HALF], F32, name="prod%d" % h)
+            for a_tile in range(2):
+                nc.tensor.matmul_mx(
+                    out=prod[:, a_tile, :],
+                    lhsT=wb_codes[:, P * a_tile : P * (a_tile + 1)].bitcast(E5M2),
+                    lhsT_scale=wb_scale[:, P * a_tile : P * (a_tile + 1)],
+                    rhs=hid_codes[:].bitcast(E5M2),
+                    rhs_scale=hid_scale[:],
+                    start=True,
+                    stop=True,
+                )
+            return prod
+
+        def add_residual(h, prod):
+            cols = slice(HALF * h, HALF * (h + 1))
+            for a_tile in range(2):
+                nc.vector.tensor_tensor(
+                    summed[:, a_tile, cols], prod[:, a_tile, :], residual[:, a_tile, cols], ALU.add
+                )
+            for a_tile in range(2):
+                nc.vector.bn_stats(stats[:, a_tile, h, :], summed[:, a_tile, cols])
+
+        turned0 = gate(0)
+        nc.scalar.copy(
+            w_codes[:].bitcast(U16).rearrange("p (t m) -> p t m", t=PACK),
+            w_raw[:].bitcast(U16).rearrange("p (m t) -> p t m", t=PACK),
+        )
+        nc.vector.tensor_copy(
+            w_scale[:].rearrange("p (t m) -> p t m", t=PACK),
+            w_scale_raw[:].rearrange("p (m t) -> p t m", t=PACK),
+        )
+        a0 = first_product(0)
+        scaled0 = scale_gate(0, turned0)
+        prod0 = second_product(0, a0, scaled0)
+        turned1 = gate(1)
+        a1 = first_product(1)
+        scaled1 = scale_gate(1, turned1)
+        prod1 = second_product(1, a1, scaled1)
+        add_residual(0, prod0)
+        add_residual(1, prod1)
+
+        moments = sb.tile([P, 2, 2], F32, name="moments")
+        inv_spread = sb.tile([P, 2], F32, name="inv_spread")
+        for a_tile in range(2):
+            nc.vector.bn_aggr(moments[:, a_tile, :], stats[:, a_tile, :, :].rearrange("p h s -> p (h s)"))
+        nc.scalar.activation(inv_spread[:], moments[:, :, 1], ACT.Abs_reciprocal_sqrt, bias=EPS)
+        centred = [sb.tile([P, J], F32, name="centred%d" % a_tile) for a_tile in range(2)]
+        y = [sb.tile([P, J], F32, name="y%d" % a_tile) for a_tile in range(2)]
+        for a_tile in (1, 0):
+            nc.vector.tensor_scalar(
+                centred[a_tile][:], summed[:, a_tile, :], moments[:, a_tile, 0:1], None, ALU.subtract
+            )
+        nc.vector.tensor_scalar(y[0][:], centred[0][:], inv_spread[:, 0:1], None, ALU.mult)
+        nc.sync.dma_start(out=out[0:P, :], in_=y[0][:])
+        nc.scalar.activation(y[1][:], centred[1][:], ACT.Copy, scale=inv_spread[:, 1:2])
+        nc.scalar.dma_start(out=out[P:N, :], in_=y[1][:])

@@ -65,6 +65,9 @@ def tile_list_rows_joined_tabled_levelled_kernel(
         nc.gpsimd.memset(w_scale_raw[:].bitcast(I32), 0)
         nc.gpsimd.memset(wb_scale[:].bitcast(I32), 0)
         make_identity(nc, identity[:])
+        warm = sb.tile([P, 2], F32, name="warm")
+        nc.vector.memset(warm[:, 0:1], 0.0)
+        nc.scalar.activation(warm[:, 1:2], warm[:, 0:1], ACT.Sigmoid)
 
         nc.gpsimd.dma_start(out=factor[:], in_=us.rearrange("o (p t) -> p (o t)", t=PACK))
         nc.sync.dma_start(list_g[:], offs3)

@@ -22,6 +22,7 @@ P = 128
 PACK = 4
 HALF = 128
 EPS = 0.1
+SCALAR_PLANES = (0, 3)
 
 
 def tile_list_rows_joined_tabled_levelled_kernel(
@@ -80,8 +81,7 @@ def tile_list_rows_joined_tabled_levelled_kernel(
         nc.sync.dma_start(out=gates[1][:], in_=tg[HALF:J, :])
         nc.sync.dma_start(list_b[:], offs2)
         load_planes(1, xb_rows, 0, 2)
-        load_planes(1, xb_rows, 2, 1)
-        load_planes(1, xb_rows, 3, 1)
+        load_planes(1, xb_rows, 2, 2)
         nc.sync.dma_start(
             out=wb_codes[:].bitcast(I32), in_=wb_words[0].rearrange("p n t -> p (n t)").bitcast(I32)
         )
@@ -112,8 +112,15 @@ def tile_list_rows_joined_tabled_levelled_kernel(
 
         def first_product(h):
             u = sb.tile([P, HALF, PACK], BF16, name="u%d" % h, tag="shared%d" % h, align_bytes=64)
-            for i in range(PACK):
+            on_scalar = SCALAR_PLANES[h]
+            if on_scalar:
+                picked = sb.tile([P, on_scalar, HALF], F32, name="picked%d" % h)
+                for i in range(on_scalar):
+                    nc.scalar.activation(picked[:, i, :], windows[h][i].indirect(lists[h][:]), ACT.Copy)
+            for i in range(on_scalar, PACK):
                 nc.vector.tensor_copy(u[:, :, i], windows[h][i].indirect(lists[h][:]))
+            if on_scalar:
+                nc.vector.tensor_copy(u[:, :, 0:on_scalar], picked[:].rearrange("p i j -> p j i"))
             u_codes = sb.tile([P, HALF], U32, name="u_codes%d" % h, align_bytes=64)
             u_scale = sb.tile([P, HALF], U8, name="u_scale%d" % h, align_bytes=64)
             nc.vector.quantize_mx(
@@ -140,10 +147,10 @@ def tile_list_rows_joined_tabled_levelled_kernel(
             nc.vector.quantize_mx(
                 out=hid_codes[:].bitcast(E5M2), scales=hid_scale[:], in_=hid[:].rearrange("p j t -> p (j t)")
             )
-            prod = ps.tile([P, 2, HALF], F32, name="prod%d" % h)
+            prod = [ps.tile([P, HALF], F32, name="prod%d_%d" % (h, a_tile)) for a_tile in range(2)]
             for a_tile in range(2):
                 nc.tensor.matmul_mx(
-                    out=prod[:, a_tile, :],
+                    out=prod[a_tile][:],
                     lhsT=wb_codes[:, P * a_tile : P * (a_tile + 1)].bitcast(E5M2),
                     lhsT_scale=wb_scale[:, P * a_tile : P * (a_tile + 1)],
                     rhs=hid_codes[:].bitcast(E5M2),
@@ -157,7 +164,7 @@ def tile_list_rows_joined_tabled_levelled_kernel(
             cols = slice(HALF * h, HALF * (h + 1))
             for a_tile in range(2):
                 nc.vector.tensor_tensor(
-                    summed[:, a_tile, cols], prod[:, a_tile, :], residual[:, a_tile, cols], ALU.add
+                    summed[:, a_tile, cols], prod[a_tile][:], residual[:, a_tile, cols], ALU.add
                 )
             for a_tile in range(2):
                 nc.vector.bn_stats(stats[:, a_tile, h, :], summed[:, a_tile, cols])
@@ -185,14 +192,17 @@ def tile_list_rows_joined_tabled_levelled_kernel(
         inv_spread = sb.tile([P, 2], F32, name="inv_spread")
         for a_tile in range(2):
             nc.vector.bn_aggr(moments[:, a_tile, :], stats[:, a_tile, :, :].rearrange("p h s -> p (h s)"))
-        nc.scalar.activation(inv_spread[:], moments[:, :, 1], ACT.Abs_reciprocal_sqrt, bias=EPS)
-        centred = [sb.tile([P, J], F32, name="centred%d" % a_tile) for a_tile in range(2)]
-        y = [sb.tile([P, J], F32, name="y%d" % a_tile) for a_tile in range(2)]
-        for a_tile in (1, 0):
-            nc.vector.tensor_scalar(
-                centred[a_tile][:], summed[:, a_tile, :], moments[:, a_tile, 0:1], None, ALU.subtract
+            nc.scalar.activation(
+                inv_spread[:, a_tile : a_tile + 1], moments[:, a_tile, 1:2], ACT.Abs_reciprocal_sqrt, bias=EPS
             )
-        nc.vector.tensor_scalar(y[0][:], centred[0][:], inv_spread[:, 0:1], None, ALU.mult)
-        nc.sync.dma_start(out=out[0:P, :], in_=y[0][:])
-        nc.scalar.activation(y[1][:], centred[1][:], ACT.Copy, scale=inv_spread[:, 1:2])
-        nc.scalar.dma_start(out=out[P:N, :], in_=y[1][:])
+        for a_tile, queue in enumerate((nc.scalar, nc.sync)):
+            y = sb.tile([P, J], F32, name="y%d" % a_tile)
+            nc.vector.tensor_scalar(
+                y[:],
+                summed[:, a_tile, :],
+                moments[:, a_tile, 0:1],
+                inv_spread[:, a_tile : a_tile + 1],
+                ALU.subtract,
+                ALU.mult,
+            )
+            queue.dma_start(out=out[P * a_tile : P * (a_tile + 1), :], in_=y[:])

from contextlib import ExitStack

import concourse.mybir as mybir
from concourse.masks import make_identity

K, T, J, R, C, N = 512, 512, 256, 512, 1024, 256
FLOPS = 2 * K * J * R + 2 * R * N * J

F32 = mybir.dt.float32
BF16 = mybir.dt.bfloat16
I32 = mybir.dt.int32
U32 = mybir.dt.uint32
U16 = mybir.dt.uint16
U8 = mybir.dt.uint8
E4M3 = mybir.dt.float8_e4m3fn_x4
E5M2 = mybir.dt.float8_e5m2_x4
E2M1 = mybir.dt.float4_e2m1fn_x4
ALU = mybir.AluOpType
ACT = mybir.ActivationFunctionType

P = 128
PACK = 4
HALF = 128
EPS = 0.1
SCALAR_PLANES = (0, 3)


def tile_list_rows_joined_tabled_levelled_kernel(
    tc, xa, xb, w_words, w_scales, us, tg, wb_words, wb_scales, rs, offs, offs2, offs3, out
):
    nc = tc.nc
    with ExitStack() as ctx:
        sb = ctx.enter_context(tc.tile_pool(name="sb", bufs=1))
        ps = ctx.enter_context(tc.psum_pool(name="ps", bufs=1))

        list_a = sb.tile([P, HALF // 16], U16, name="list_a")
        list_b = sb.tile([P, HALF // 16], U16, name="list_b")
        list_g = sb.tile([P, R // 16], U16, name="list_g")
        gates = [sb.tile([P, C], F32, name="gates%d" % h) for h in range(2)]
        w_raw = sb.tile([P, 2 * R], U8, name="w_raw")
        w_scale_raw = sb.tile([P, R], U8, name="w_scale_raw")
        w_codes = sb.tile([P, 2 * R], U8, name="w_codes", align_bytes=64)
        w_scale = sb.tile([P, R], U8, name="w_scale", align_bytes=64)
        wb_codes = sb.tile([P, N], U32, name="wb_codes", align_bytes=64)
        wb_scale = sb.tile([P, N], U8, name="wb_scale", align_bytes=64)
        factor = sb.tile([P, PACK], F32, name="factor")
        residual = sb.tile([P, 2, J], F32, name="residual")
        identity = sb.tile([P, P], F32, name="identity")

        xa_rows = xa.rearrange("(p i) t -> p i t", i=PACK)
        xb_rows = xb.rearrange("(p i) t -> p i t", i=PACK)
        windows = [[], []]

        def load_planes(h, rows, first, count):
            tile = sb.tile([P, count, T], F32, name="x%d_%d" % (h, first))
            nc.sync.dma_start(out=tile[:], in_=rows[:, first : first + count, :])
            for i in range(count):
                windows[h].append(tile[:, i, :])

        def load_scale_rows(plane, rows):
            for q in range(4):
                nc.sync.dma_start(
                    out=plane[32 * q : 32 * q + 4, :].bitcast(I32), in_=rows[0, 4 * q : 4 * q + 4, :].bitcast(I32)
                )

        nc.gpsimd.memset(w_scale_raw[:].bitcast(I32), 0)
        nc.gpsimd.memset(wb_scale[:].bitcast(I32), 0)
        make_identity(nc, identity[:])
        warm = sb.tile([P, 2], F32, name="warm")
        nc.vector.memset(warm[:, 0:1], 0.0)
        nc.scalar.activation(warm[:, 1:2], warm[:, 0:1], ACT.Sigmoid)

        nc.gpsimd.dma_start(out=factor[:], in_=us.rearrange("o (p t) -> p (o t)", t=PACK))
        nc.sync.dma_start(list_g[:], offs3)
        nc.sync.dma_start(out=gates[0][:], in_=tg[0:HALF, :])
        load_scale_rows(w_scale_raw, w_scales)
        nc.sync.dma_start(list_a[:], offs)
        load_planes(0, xa_rows, 0, 2)
        load_planes(0, xa_rows, 2, 2)
        nc.sync.dma_start(out=w_raw[:].bitcast(I32), in_=w_words[0].bitcast(I32))
        nc.sync.dma_start(out=gates[1][:], in_=tg[HALF:J, :])
        nc.sync.dma_start(list_b[:], offs2)
        load_planes(1, xb_rows, 0, 2)
        load_planes(1, xb_rows, 2, 2)
        nc.sync.dma_start(
            out=wb_codes[:].bitcast(I32), in_=wb_words[0].rearrange("p n t -> p (n t)").bitcast(I32)
        )
        load_scale_rows(wb_scale, wb_scales)
        nc.sync.dma_start(out=residual[:], in_=rs.rearrange("(a p) j -> p a j", p=P))

        summed = sb.tile([P, 2, J], F32, name="summed")
        stats = sb.tile([P, 2, 2, 6], F32, name="stats")
        lists = [list_a, list_b]

        def gate(h):
            sig = sb.tile([P, R], F32, name="sig%d" % h)
            nc.scalar.activation(sig[:], gates[h][:].indirect(list_g[:]), ACT.Sigmoid)
            turned = ps.tile([P, PACK, HALF], F32, name="turned%d" % h)
            for t in range(PACK):
                nc.tensor.transpose(turned[:, t, :], sig[:, t:R:PACK], identity[:])
            return turned

        def scale_gate(h, turned):
            scaled = sb.tile([P, HALF, PACK], F32, name="scaled%d" % h, tag="shared%d" % h, align_bytes=64)
            nc.vector.tensor_tensor(
                scaled[:],
                turned[:].rearrange("p t j -> p j t"),
                factor[:].unsqueeze(1).to_broadcast([P, HALF, PACK]),
                ALU.mult,
            )
            return scaled

        def first_product(h):
            u = sb.tile([P, HALF, PACK], BF16, name="u%d" % h, tag="shared%d" % h, align_bytes=64)
            on_scalar = SCALAR_PLANES[h]
            if on_scalar:
                picked = sb.tile([P, on_scalar, HALF], F32, name="picked%d" % h)
                for i in range(on_scalar):
                    nc.scalar.activation(picked[:, i, :], windows[h][i].indirect(lists[h][:]), ACT.Copy)
            for i in range(on_scalar, PACK):
                nc.vector.tensor_copy(u[:, :, i], windows[h][i].indirect(lists[h][:]))
            if on_scalar:
                nc.vector.tensor_copy(u[:, :, 0:on_scalar], picked[:].rearrange("p i j -> p j i"))
            u_codes = sb.tile([P, HALF], U32, name="u_codes%d" % h, align_bytes=64)
            u_scale = sb.tile([P, HALF], U8, name="u_scale%d" % h, align_bytes=64)
            nc.vector.quantize_mx(
                out=u_codes[:].bitcast(E4M3), scales=u_scale[:], in_=u[:].rearrange("p j i -> p (j i)")
            )
            a = ps.tile([P, PACK, HALF], F32, name="a%d" % h)
            for t in range(PACK):
                nc.tensor.matmul_mx(
                    out=a[:, t, :],
                    lhsT=w_codes[:, 2 * P * t : 2 * P * (t + 1)].bitcast(E2M1),
                    lhsT_scale=w_scale[:, P * t : P * (t + 1)],
                    rhs=u_codes[:].bitcast(E4M3),
                    rhs_scale=u_scale[:],
                    start=True,
                    stop=True,
                )
            return a

        def second_product(h, a, scaled):
            hid = sb.tile([P, HALF, PACK], BF16, name="hid%d" % h, align_bytes=64)
            nc.vector.tensor_tensor(hid[:], a[:].rearrange("p t j -> p j t"), scaled[:], ALU.mult)
            hid_codes = sb.tile([P, HALF], U32, name="hid_codes%d" % h, align_bytes=64)
            hid_scale = sb.tile([P, HALF], U8, name="hid_scale%d" % h, align_bytes=64)
            nc.vector.quantize_mx(
                out=hid_codes[:].bitcast(E5M2), scales=hid_scale[:], in_=hid[:].rearrange("p j t -> p (j t)")
            )
            prod = [ps.tile([P, HALF], F32, name="prod%d_%d" % (h, a_tile)) for a_tile in range(2)]
            for a_tile in range(2):
                nc.tensor.matmul_mx(
                    out=prod[a_tile][:],
                    lhsT=wb_codes[:, P * a_tile : P * (a_tile + 1)].bitcast(E5M2),
                    lhsT_scale=wb_scale[:, P * a_tile : P * (a_tile + 1)],
                    rhs=hid_codes[:].bitcast(E5M2),
                    rhs_scale=hid_scale[:],
                    start=True,
                    stop=True,
                )
            return prod

        def add_residual(h, prod):
            cols = slice(HALF * h, HALF * (h + 1))
            for a_tile in range(2):
                nc.vector.tensor_tensor(
                    summed[:, a_tile, cols], prod[a_tile][:], residual[:, a_tile, cols], ALU.add
                )
            for a_tile in range(2):
                nc.vector.bn_stats(stats[:, a_tile, h, :], summed[:, a_tile, cols])

        turned0 = gate(0)
        nc.scalar.copy(
            w_codes[:].bitcast(U16).rearrange("p (t m) -> p t m", t=PACK),
            w_raw[:].bitcast(U16).rearrange("p (m t) -> p t m", t=PACK),
        )
        nc.vector.tensor_copy(
            w_scale[:].rearrange("p (t m) -> p t m", t=PACK),
            w_scale_raw[:].rearrange("p (m t) -> p t m", t=PACK),
        )
        a0 = first_product(0)
        scaled0 = scale_gate(0, turned0)
        prod0 = second_product(0, a0, scaled0)
        turned1 = gate(1)
        a1 = first_product(1)
        scaled1 = scale_gate(1, turned1)
        prod1 = second_product(1, a1, scaled1)
        add_residual(0, prod0)
        add_residual(1, prod1)

        moments = sb.tile([P, 2, 2], F32, name="moments")
        inv_spread = sb.tile([P, 2], F32, name="inv_spread")
        for a_tile in range(2):
            nc.vector.bn_aggr(moments[:, a_tile, :], stats[:, a_tile, :, :].rearrange("p h s -> p (h s)"))
            nc.scalar.activation(
                inv_spread[:, a_tile : a_tile + 1], moments[:, a_tile, 1:2], ACT.Abs_reciprocal_sqrt, bias=EPS
            )
        for a_tile, queue in enumerate((nc.scalar, nc.sync)):
            y = sb.tile([P, J], F32, name="y%d" % a_tile)
            nc.vector.tensor_scalar(
                y[:],
                summed[:, a_tile, :],
                moments[:, a_tile, 0:1],
                inv_spread[:, a_tile : a_tile + 1],
                ALU.subtract,
                ALU.mult,
            )
            queue.dma_start(out=out[P * a_tile : P * (a_tile + 1), :], in_=y[:])
